import numpy as np
CORES = [0,1,2,3]
N = 4
def setup_inputs(rng):
    return {"x": rng.standard_normal((N, 128, 64), dtype=np.float32)}
def reference(x):
    g = np.ascontiguousarray(x.transpose(1, 2, 0)).reshape(128, 64 * N)
    return {"y": np.broadcast_to(g, (N,) + g.shape)}

@@ -1,0 +1,56 @@
+from concourse.bass import DstId, RemoteDMATransfer
+
+N = 4
+COLS = 64
+BLK = COLS // N
+
+SCRATCH = {
+    "xs": ("sbuf", [128, COLS], "float32"),
+    "land": ("sbuf", [128, N, BLK], "float32"),
+    "out": ("sbuf", [128, COLS, N], "float32"),
+}
+SEMAPHORES = ["loaded", "pieces", "spread", "blocks", "sent", "stored"]
+
+
+def rank_program(g, core, T, topo):
+    r = T.rank_of(core)
+    if r is None:
+        return
+    sem = T.sem
+    peers = [s for s in range(N) if s != r]
+
+    def dst_id(s):
+        rid, pid, _se = topo.addr(T.cores[s])
+        return DstId(rid=rid, pnc=pid)
+
+    mine = slice(BLK * r, BLK * (r + 1))
+
+    def spread(s, piece):
+        g.dma_start(T.out[:, mine, s], piece, allow_slow_non_contiguous=True).then_inc(sem.spread, 16)
+
+    g.sync.dma_start(T.xs[:], T.x[:]).then_inc(sem.loaded, 16)
+    spread(r, T.x[:, mine])
+
+    g.wait_ge(sem.loaded, 16)
+    g.remote_dma_fused(
+        [RemoteDMATransfer(dst_ids=[dst_id(d)], dma_engine_mask=0xF << (4 * k), remote_sem=sem.pieces,
+                           src=T.xs[:, BLK * d:BLK * (d + 1)], dst=T.land[:, r, :])
+         for k, d in enumerate(peers)],
+        local_sem=sem.sent)
+
+    g.wait_ge(sem.pieces, 12)
+    for s in peers:
+        spread(s, T.land[:, s, :])
+
+    g.wait_ge(sem.spread, 64)
+    g.remote_dma_fused(
+        [RemoteDMATransfer(dst_ids=[dst_id(d) for d in peers], dma_engine_mask=topo.mask(core, T.cores[peers[0]]),
+                           remote_sem=sem.blocks, srcs=[T.out[:, mine, :]], dsts=[T.out[:, mine, :] for _d in peers])],
+        local_sem=sem.sent)
+
+    g.wait_ge(sem.blocks, 48)
+    g.sync.wait_ge(sem.blocks, 48)
+    g.sync.wait_ge(sem.spread, 64)
+    g.sync.dma_start(T.y[:], T.out[:]).then_inc(sem.stored, 16)
+    g.wait_ge(sem.stored, 16)
+    g.wait_ge(sem.sent, 28)

@@ -1,8 +1,9 @@
 from concourse.bass import DstId, RemoteDMATransfer
 
 N = 4
+W = 8
 COLS = 64
-BLK = COLS // N
+BLK = COLS // W
 
 SCRATCH = {
     "xs": ("sbuf", [128, COLS], "float32"),
@@ -13,44 +14,51 @@ SEMAPHORES = ["loaded", "pieces", "spread", "blocks", "sent", "stored"]
 
 
 def rank_program(g, core, T, topo):
-    r = T.rank_of(core)
-    if r is None:
-        return
     sem = T.sem
-    peers = [s for s in range(N) if s != r]
+    ranks = list(T.cores)
+    workers = ranks + [c for c in range(W) if c not in ranks]
+    w = workers.index(core)
+    r = T.rank_of(core)
 
-    def dst_id(s):
-        rid, pid, _se = topo.addr(T.cores[s])
+    def dst_id(c):
+        rid, pid, _se = topo.addr(c)
         return DstId(rid=rid, pnc=pid)
 
-    mine = slice(BLK * r, BLK * (r + 1))
+    mine = slice(BLK * w, BLK * (w + 1))
 
     def spread(s, piece):
         g.dma_start(T.out[:, mine, s], piece, allow_slow_non_contiguous=True).then_inc(sem.spread, 16)
 
-    g.sync.dma_start(T.xs[:], T.x[:]).then_inc(sem.loaded, 16)
-    spread(r, T.x[:, mine])
+    sent = 0
+    if r is not None:
+        g.sync.dma_start(T.xs[:], T.x[:]).then_inc(sem.loaded, 16)
+        spread(r, T.x[:, mine])
 
-    g.wait_ge(sem.loaded, 16)
-    g.remote_dma_fused(
-        [RemoteDMATransfer(dst_ids=[dst_id(d)], dma_engine_mask=0xF << (4 * k), remote_sem=sem.pieces,
-                           src=T.xs[:, BLK * d:BLK * (d + 1)], dst=T.land[:, r, :])
-         for k, d in enumerate(peers)],
-        local_sem=sem.sent)
+        g.wait_ge(sem.loaded, 16)
+        others = [v for v in range(W) if v != w]
+        g.remote_dma_fused(
+            [RemoteDMATransfer(dst_ids=[dst_id(workers[v])], dma_engine_mask=0x3 << (2 * k), remote_sem=sem.pieces,
+                               src=T.xs[:, BLK * v:BLK * (v + 1)], dst=T.land[:, r, :])
+             for k, v in enumerate(others)],
+            local_sem=sem.sent)
+        sent += 2 * len(others)
 
-    g.wait_ge(sem.pieces, 12)
-    for s in peers:
+    senders = [s for s in range(N) if s != r]
+    g.wait_ge(sem.pieces, 2 * len(senders))
+    for s in senders:
         spread(s, T.land[:, s, :])
 
-    g.wait_ge(sem.spread, 64)
+    g.wait_ge(sem.spread, 16 * N)
+    takers = [c for c in ranks if c != core]
     g.remote_dma_fused(
-        [RemoteDMATransfer(dst_ids=[dst_id(d) for d in peers], dma_engine_mask=topo.mask(core, T.cores[peers[0]]),
-                           remote_sem=sem.blocks, srcs=[T.out[:, mine, :]], dsts=[T.out[:, mine, :] for _d in peers])],
+        [RemoteDMATransfer(dst_ids=[dst_id(c) for c in takers], dma_engine_mask=topo.mask(core, takers[0]),
+                           remote_sem=sem.blocks, srcs=[T.out[:, mine, :]], dsts=[T.out[:, mine, :] for _c in takers])],
         local_sem=sem.sent)
+    sent += 16
 
-    g.wait_ge(sem.blocks, 48)
-    g.sync.wait_ge(sem.blocks, 48)
-    g.sync.wait_ge(sem.spread, 64)
-    g.sync.dma_start(T.y[:], T.out[:]).then_inc(sem.stored, 16)
-    g.wait_ge(sem.stored, 16)
-    g.wait_ge(sem.sent, 28)
+    if r is not None:
+        g.sync.wait_ge(sem.blocks, 16 * (W - 1))
+        g.sync.wait_ge(sem.spread, 16 * N)
+        g.sync.dma_start(T.y[:], T.out[:]).then_inc(sem.stored, 16)
+        g.wait_ge(sem.stored, 16)
+    g.wait_ge(sem.sent, sent)

from concourse.bass import DstId, RemoteDMATransfer

N = 4
W = 8
COLS = 64
BLK = COLS // W

SCRATCH = {
    "xs": ("sbuf", [128, COLS], "float32"),
    "land": ("sbuf", [128, N, BLK], "float32"),
    "out": ("sbuf", [128, COLS, N], "float32"),
}
SEMAPHORES = ["loaded", "pieces", "spread", "blocks", "sent", "stored"]


def rank_program(g, core, T, topo):
    sem = T.sem
    ranks = list(T.cores)
    workers = ranks + [c for c in range(W) if c not in ranks]
    w = workers.index(core)
    r = T.rank_of(core)

    def dst_id(c):
        rid, pid, _se = topo.addr(c)
        return DstId(rid=rid, pnc=pid)

    mine = slice(BLK * w, BLK * (w + 1))

    def spread(s, piece):
        g.dma_start(T.out[:, mine, s], piece, allow_slow_non_contiguous=True).then_inc(sem.spread, 16)

    sent = 0
    if r is not None:
        g.sync.dma_start(T.xs[:], T.x[:]).then_inc(sem.loaded, 16)
        spread(r, T.x[:, mine])

        g.wait_ge(sem.loaded, 16)
        others = [v for v in range(W) if v != w]
        g.remote_dma_fused(
            [RemoteDMATransfer(dst_ids=[dst_id(workers[v])], dma_engine_mask=0x3 << (2 * k), remote_sem=sem.pieces,
                               src=T.xs[:, BLK * v:BLK * (v + 1)], dst=T.land[:, r, :])
             for k, v in enumerate(others)],
            local_sem=sem.sent)
        sent += 2 * len(others)

    senders = [s for s in range(N) if s != r]
    g.wait_ge(sem.pieces, 2 * len(senders))
    for s in senders:
        spread(s, T.land[:, s, :])

    g.wait_ge(sem.spread, 16 * N)
    takers = [c for c in ranks if c != core]
    g.remote_dma_fused(
        [RemoteDMATransfer(dst_ids=[dst_id(c) for c in takers], dma_engine_mask=topo.mask(core, takers[0]),
                           remote_sem=sem.blocks, srcs=[T.out[:, mine, :]], dsts=[T.out[:, mine, :] for _c in takers])],
        local_sem=sem.sent)
    sent += 16

    if r is not None:
        g.sync.wait_ge(sem.blocks, 16 * (W - 1))
        g.sync.wait_ge(sem.spread, 16 * N)
        g.sync.dma_start(T.y[:], T.out[:]).then_inc(sem.stored, 16)
        g.wait_ge(sem.stored, 16)
    g.wait_ge(sem.sent, sent)
